import numpy as np
import ml_dtypes


def mxq(x, axis, fmt="e4m3"):
    dtype, down = {"e4m3": (ml_dtypes.float8_e4m3fn, 7), "e5m2": (ml_dtypes.float8_e5m2, 14)}[fmt]
    v = np.moveaxis(np.asarray(x, np.float32).astype(ml_dtypes.bfloat16).astype(np.float64), axis, -1)
    blocks = v.reshape(v.shape[:-1] + (-1, 32))
    amax = np.abs(blocks).max(-1, keepdims=True)
    byte = np.maximum(np.where(amax > 0, np.frexp(amax)[1] - 1 + 127, 0) - down, 1)
    scale = np.exp2(byte - 127.0)
    codes = (blocks / scale).astype(np.float32).astype(dtype).astype(np.float64)
    return np.moveaxis((codes * scale).reshape(v.shape), -1, axis)


WIDE = False


def mx_kscale(k, group=512):
    if not WIDE:
        return np.ones(k)
    levels = np.array([18, -18])
    if group != 512:
        return np.exp2(np.random.permutation(np.resize(levels, k // group))).repeat(group)
    if k % 512:
        return np.exp2(np.random.permutation(np.resize(levels, k // 32))).repeat(32)
    a = np.empty((k // 512, 16))
    for p in range(k // 512):
        a[p, :8] = np.random.permutation(np.resize(levels, 8))
        for g in range(8):
            far = levels[np.abs(levels - a[p, g]) >= 10]
            a[p, g + 8] = far[np.random.randint(len(far))]
    return np.exp2(a.ravel()).repeat(32)


def f64(x):
    return np.asarray(x).astype(np.float64)


G, D, M, O, N = 4, 128, 128, 128, 512


def setup_inputs():
    n = np.random.standard_normal
    s_d = mx_kscale(D, 0)
    s_o = mx_kscale(O, 0)
    return {
        "x": (n((G, D, N)) * s_d[:, None]).astype(np.float32),
        "w1": (n((G, D, M)) / np.sqrt(D) / s_d[:, None]).astype(np.float32),
        "w2": (n((G, D, M)) / np.sqrt(D) / s_d[:, None]).astype(np.float32),
        "w3": (n((G, D, M)) / np.sqrt(D) / s_d[:, None]).astype(np.float32),
        "re": (np.random.uniform(0.3, 1.5, (G, M, 1))).astype(np.float32),
        "wo": (n((G, O, M)) / np.sqrt(O) / s_o[:, None]).astype(np.float32),
        "dy": (n((G, O, N)) * s_o[:, None]).astype(np.float32),
        "old": (0.3 * n((G, M, N))).astype(np.float32),
    }


def reference(x, w1, w2, w3, re, wo, dy, old):
    w1q = mxq(f64(w1), 1, "e4m3")
    xq = mxq(f64(x), 1, "e4m3")
    z1 = w1q.transpose(0, 2, 1) @ xq
    w2q = mxq(f64(w2), 1, "e4m3")
    z2 = w2q.transpose(0, 2, 1) @ xq
    w3q = mxq(f64(w3), 1, "e4m3")
    z3 = w3q.transpose(0, 2, 1) @ xq
    e1 = np.exp(z1)
    e2 = np.exp(z2)
    woq = mxq(f64(wo), 1, "e4m3")
    dyq = mxq(f64(dy), 1, "e4m3")
    c0 = woq.transpose(0, 2, 1) @ dyq
    de1 = c0 * z3 / (e1 + e2 + f64(re)) - c0 * z3 * e1 / np.square(e1 + e2 + f64(re))
    dz1 = de1 * e1
    y = dz1 + f64(old)
    return y

@@ -1,0 +1,190 @@
+from contextlib import ExitStack
+
+import concourse.mybir as mybir
+
+G, D, M, N = 4, 128, 128, 512
+FLOPS = 4 * 2 * G * D * M * N
+
+F32 = mybir.dt.float32
+BF16 = mybir.dt.bfloat16
+U32 = mybir.dt.uint32
+U8 = mybir.dt.uint8
+FP8X4 = mybir.dt.float8_e4m3fn_x4
+ACT = mybir.ActivationFunctionType
+ALU = mybir.AluOpType
+
+P = 128
+PACK = 4
+ROWS = D // PACK
+HALF = N // 2
+X_SPLIT = 336
+
+
+def tile_rows_btwoshare_kernel(tc, x, w1, w2, w3, re, wo, dy, old, out):
+    nc = tc.nc
+    with ExitStack() as ctx:
+        sb = ctx.enter_context(tc.tile_pool(name="sb", bufs=1))
+        ps = ctx.enter_context(tc.psum_pool(name="ps", bufs=1))
+        ctx.enter_context(tc.manual_schedule())
+
+        def load(name, src, width):
+            raw = sb.tile([P, PACK, width], F32, name=name + "_raw", align_bytes=64)
+            nc.sync.dma_start(out=raw[:], in_=src.rearrange("g (p j) c -> (g p) j c", j=PACK))
+            return raw
+
+        def views(grouped, at, raw, c0, c1):
+            dst = grouped[:, at + c0 : at + c1, :].rearrange("p (c i) j -> p c j i", i=4)
+            src = raw[:, :, c0:c1].rearrange("p j (c i) -> p c j i", i=4)
+            return dst, src
+
+        def operand(name, width):
+            grouped = sb.tile([P, width, PACK], BF16, name=name + "_bf16", align_bytes=64)
+            codes = sb.tile([P, width], U32, name=name + "_codes", align_bytes=64)
+            scales = sb.tile([P, width], U8, name=name + "_scales", align_bytes=64)
+            return grouped, codes, scales
+
+        def quantize(op, c0, c1):
+            grouped, codes, scales = op
+            nc.vector.quantize_mx(
+                out=codes[:, c0:c1].bitcast(FP8X4),
+                scales=scales[:, c0:c1],
+                in_=grouped[:, c0:c1, :].rearrange("p c j -> p (c j)"),
+            )
+
+        def product(bank, g, wop, at, mop, start, stop):
+            r = slice(ROWS * g, ROWS * (g + 1))
+            nc.tensor.matmul_mx(
+                out=bank[:],
+                lhsT=wop[1][r, at : at + M].bitcast(FP8X4),
+                lhsT_scale=wop[2][r, at : at + M],
+                rhs=mop[1][r, :].bitcast(FP8X4),
+                rhs_scale=mop[2][r, :],
+                start=start,
+                stop=stop,
+            )
+
+        def work(name):
+            return [sb.tile([P, N], F32, name="%s%d" % (name, g), align_bytes=64) for g in range(G)]
+
+        re_rows = sb.tile([P, G * 32], F32, name="re_rows", align_bytes=64)
+        re_cols = sb.tile([P, G * 32], F32, name="re_cols", align_bytes=64)
+        nc.vector.memset(re_rows[:], 0.0)
+        nc.scalar.dma_start(
+            out=re_rows[0:P:32, :].rearrange("q (g i) -> q g i", g=G),
+            in_=re.rearrange("g (q i) o -> q g (i o)", i=32),
+        )
+
+        w1_raw = load("w1", w1, M)
+        x_raw = load("x", x, N)
+        w2_raw = load("w2", w2, M)
+        w3_raw = load("w3", w3, M)
+        wo_raw = load("wo", wo, M)
+        dy_raw = load("dy", dy, N)
+        old_sb = sb.tile([P, G, N], F32, name="old_sb", align_bytes=64)
+        nc.sync.dma_start(out=old_sb[:], in_=old.rearrange("g m n -> m g n"))
+
+        w1q = operand("w1", M)
+        w2q = operand("w2", M)
+        w3oq = operand("w3o", 2 * M)
+        xq = operand("x", N)
+        dyq = operand("dy", N)
+        bank_a = [ps.tile([P, N], F32, name="bank_a%d" % g) for g in range(G)]
+        bank_b = [ps.tile([P, N], F32, name="bank_b%d" % g) for g in range(G)]
+        e_z = work("e_z")
+        e_d = work("e_d")
+        odds = work("odds")
+        sq = work("sq")
+        share = work("share")
+        dev = work("dev")
+        m1 = work("m1")
+        m2 = work("m2")
+        y = work("y")
+
+        dst, src = views(w1q[0], 0, w1_raw, 0, M)
+        nc.vector.tensor_scalar(out=dst, in0=src, scalar1=-1.0, scalar2=None, op0=ALU.mult)
+        nc.vector.transpose(out=re_cols[:], in_=re_rows[:])
+        quantize(w1q, 0, M)
+
+        dst, src = views(xq[0], 0, x_raw, X_SPLIT, N)
+        nc.scalar.copy(out=dst, in_=src)
+        dst, src = views(xq[0], 0, x_raw, 0, HALF)
+        nc.vector.tensor_copy(out=dst, in_=src)
+        dst, src = views(xq[0], 0, x_raw, HALF, X_SPLIT)
+        nc.vector.tensor_copy(out=dst, in_=src)
+        quantize(xq, 0, HALF)
+        quantize(xq, HALF, N)
+        dst, src = views(w2q[0], 0, w2_raw, 0, M)
+        nc.vector.tensor_copy(out=dst, in_=src)
+        dst, src = views(w3oq[0], 0, w3_raw, 0, M)
+        nc.vector.tensor_copy(out=dst, in_=src)
+        quantize(w2q, 0, M)
+        dst, src = views(w3oq[0], M, wo_raw, 0, M)
+        nc.vector.tensor_copy(out=dst, in_=src)
+
+        for g in range(G):
+            product(bank_b[g], g, w1q, 0, xq, True, True)
+        for g in range(G):
+            product(bank_a[g], g, w1q, 0, xq, True, False)
+        for g in range(G):
+            product(bank_a[g], g, w2q, 0, xq, False, True)
+
+        def exp_z(g):
+            nc.scalar.activation(out=e_z[g][:], in_=bank_b[g][:], func=ACT.Exp)
+
+        def exp_d(g):
+            nc.scalar.activation(out=e_d[g][:], in_=bank_a[g][:], func=ACT.Exp)
+
+        def make_odds(g):
+            nc.vector.scalar_tensor_tensor(
+                out=odds[g][:], in0=e_z[g][:], scalar=re_cols[:, 32 * g : 32 * g + 1], in1=e_d[g][:],
+                op0=ALU.mult, op1=ALU.add)
+
+        def make_sq(g):
+            nc.vector.scalar_tensor_tensor(
+                out=sq[g][:], in0=odds[g][:], scalar=2.0, in1=odds[g][:], op0=ALU.add, op1=ALU.mult)
+
+        def cast_dy(h):
+            dst, src = views(dyq[0], 0, dy_raw, h * HALF, (h + 1) * HALF)
+            nc.vector.tensor_copy(out=dst, in_=src)
+
+        exp_z(0)
+        exp_z(1)
+        exp_d(0)
+        exp_d(1)
+        exp_z(2)
+        exp_d(2)
+        exp_z(3)
+        exp_d(3)
+        quantize(w3oq, 0, 2 * M)
+        make_odds(0)
+        cast_dy(0)
+        make_odds(1)
+        cast_dy(1)
+        make_sq(0)
+        quantize(dyq, 0, N)
+        make_odds(2)
+        make_sq(1)
+        make_odds(3)
+        make_sq(2)
+        make_sq(3)
+        for g in range(G):
+            product(bank_a[g], g, w3oq, 0, xq, True, True)
+        for g in range(G):
+            product(bank_b[g], g, w3oq, M, dyq, True, True)
+
+        halves = [slice(0, HALF), slice(HALF, N)]
+        for g in range(G):
+            for c in halves:
+                nc.scalar.activation(out=share[g][:, c], in_=sq[g][:, c], func=ACT.Abs_reciprocal_sqrt, bias=1.0)
+            for c in halves:
+                nc.scalar.activation(out=dev[g][:, c], in_=share[g][:, c], func=ACT.Square, bias=-0.5)
+            for c in halves:
+                nc.vector.scalar_tensor_tensor(
+                    out=m1[g][:, c], in0=dev[g][:, c], scalar=0.25, in1=bank_a[g][:, c],
+                    op0=ALU.subtract, op1=ALU.mult)
+            for c in halves:
+                nc.vector.tensor_tensor(out=m2[g][:, c], in0=m1[g][:, c], in1=bank_b[g][:, c], op=ALU.mult)
+            eng = nc.gpsimd if g < G - 1 else nc.vector
+            for c in halves:
+                eng.tensor_tensor(out=y[g][:, c], in0=old_sb[:, g, c], in1=m2[g][:, c], op=ALU.subtract)
+            nc.sync.dma_start(out=out[g], in_=y[g][:])

@@ -16,8 +16,16 @@ ALU = mybir.AluOpType
 P = 128
 PACK = 4
 ROWS = D // PACK
+BLOCK = 32
 HALF = N // 2
-X_SPLIT = 336
+QUARTER = N // 4
+X_VECTOR_COLUMNS = 160
+
+PIECES = [(0, slice(0, QUARTER)), (0, slice(QUARTER, HALF)), (0, slice(HALF, N))] + [
+    (g, slice(h * HALF, (h + 1) * HALF)) for g in range(1, G) for h in range(2)
+]
+SCALAR_SQUARES = 3
+VECTOR_FINISHES = 2
 
 
 def tile_rows_btwoshare_kernel(tc, x, w1, w2, w3, re, wo, dy, old, out):
@@ -27,164 +35,175 @@ def tile_rows_btwoshare_kernel(tc, x, w1, w2, w3, re, wo, dy, old, out):
         ps = ctx.enter_context(tc.psum_pool(name="ps", bufs=1))
         ctx.enter_context(tc.manual_schedule())
 
-        def load(name, src, width):
-            raw = sb.tile([P, PACK, width], F32, name=name + "_raw", align_bytes=64)
-            nc.sync.dma_start(out=raw[:], in_=src.rearrange("g (p j) c -> (g p) j c", j=PACK))
+        def load(name, src, first, last):
+            raw = sb.tile([P, PACK, last - first], F32, name=name + "_raw", align_bytes=64)
+            nc.sync.dma_start(out=raw[:], in_=src.rearrange("g (p j) c -> (g p) j c", j=PACK)[:, :, first:last])
             return raw
 
-        def views(grouped, at, raw, c0, c1):
-            dst = grouped[:, at + c0 : at + c1, :].rearrange("p (c i) j -> p c j i", i=4)
-            src = raw[:, :, c0:c1].rearrange("p j (c i) -> p c j i", i=4)
-            return dst, src
-
         def operand(name, width):
-            grouped = sb.tile([P, width, PACK], BF16, name=name + "_bf16", align_bytes=64)
+            rounded = sb.tile([P, width, PACK], BF16, name=name + "_bf16", align_bytes=64)
             codes = sb.tile([P, width], U32, name=name + "_codes", align_bytes=64)
             scales = sb.tile([P, width], U8, name=name + "_scales", align_bytes=64)
-            return grouped, codes, scales
+            return rounded, codes, scales
 
-        def quantize(op, c0, c1):
-            grouped, codes, scales = op
+        def round_to_bf16(copy, mx, at, raw, first, last):
+            copy(
+                out=mx[0][:, at + first : at + last, :].rearrange("p (c i) j -> p c j i", i=2),
+                in_=raw[:, :, first:last].rearrange("p j (c i) -> p c j i", i=2),
+            )
+
+        def quantize(mx, first, last):
+            rounded, codes, scales = mx
             nc.vector.quantize_mx(
-                out=codes[:, c0:c1].bitcast(FP8X4),
-                scales=scales[:, c0:c1],
-                in_=grouped[:, c0:c1, :].rearrange("p c j -> p (c j)"),
+                out=codes[:, first:last].bitcast(FP8X4),
+                scales=scales[:, first:last],
+                in_=rounded[:, first:last, :].rearrange("p c j -> p (c j)"),
             )
 
-        def product(bank, g, wop, at, mop, start, stop):
-            r = slice(ROWS * g, ROWS * (g + 1))
+        def product(bank, g, weights, at, moving):
+            rows = slice(ROWS * g, ROWS * (g + 1))
             nc.tensor.matmul_mx(
-                out=bank[:],
-                lhsT=wop[1][r, at : at + M].bitcast(FP8X4),
-                lhsT_scale=wop[2][r, at : at + M],
-                rhs=mop[1][r, :].bitcast(FP8X4),
-                rhs_scale=mop[2][r, :],
-                start=start,
-                stop=stop,
+                out=bank[g][:],
+                lhsT=weights[1][rows, at : at + M].bitcast(FP8X4),
+                lhsT_scale=weights[2][rows, at : at + M],
+                rhs=moving[1][rows, :].bitcast(FP8X4),
+                rhs_scale=moving[2][rows, :],
+                start=True,
+                stop=True,
             )
 
-        def work(name):
+        def per_group(name):
             return [sb.tile([P, N], F32, name="%s%d" % (name, g), align_bytes=64) for g in range(G)]
 
-        re_rows = sb.tile([P, G * 32], F32, name="re_rows", align_bytes=64)
-        re_cols = sb.tile([P, G * 32], F32, name="re_cols", align_bytes=64)
-        nc.vector.memset(re_rows[:], 0.0)
+        re_rows = sb.tile([P, G * BLOCK], F32, name="re_rows", align_bytes=64)
+        re_cols = sb.tile([P, G * BLOCK], F32, name="re_cols", align_bytes=64)
+        nc.gpsimd.memset(re_rows[:], 0.0)
         nc.scalar.dma_start(
-            out=re_rows[0:P:32, :].rearrange("q (g i) -> q g i", g=G),
-            in_=re.rearrange("g (q i) o -> q g (i o)", i=32),
+            out=re_rows[0:P:BLOCK, :].rearrange("q (g i) -> q g i", g=G),
+            in_=re.rearrange("g (q i) o -> q g (i o)", i=BLOCK),
         )
 
-        w1_raw = load("w1", w1, M)
-        x_raw = load("x", x, N)
-        w2_raw = load("w2", w2, M)
-        w3_raw = load("w3", w3, M)
-        wo_raw = load("wo", wo, M)
-        dy_raw = load("dy", dy, N)
+        w1_raw = load("w1", w1, 0, M)
+        x_raw = [load("x0", x, 0, HALF), load("x1", x, HALF, N)]
+        w2_raw = load("w2", w2, 0, M)
+        w3_raw = load("w3", w3, 0, M)
+        wo_raw = load("wo", wo, 0, M)
+        dy_raw = load("dy", dy, 0, N)
         old_sb = sb.tile([P, G, N], F32, name="old_sb", align_bytes=64)
         nc.sync.dma_start(out=old_sb[:], in_=old.rearrange("g m n -> m g n"))
 
-        w1q = operand("w1", M)
-        w2q = operand("w2", M)
-        w3oq = operand("w3o", 2 * M)
-        xq = operand("x", N)
-        dyq = operand("dy", N)
-        bank_a = [ps.tile([P, N], F32, name="bank_a%d" % g) for g in range(G)]
-        bank_b = [ps.tile([P, N], F32, name="bank_b%d" % g) for g in range(G)]
-        e_z = work("e_z")
-        e_d = work("e_d")
-        odds = work("odds")
-        sq = work("sq")
-        share = work("share")
-        dev = work("dev")
-        m1 = work("m1")
-        m2 = work("m2")
-        y = work("y")
-
-        dst, src = views(w1q[0], 0, w1_raw, 0, M)
-        nc.vector.tensor_scalar(out=dst, in0=src, scalar1=-1.0, scalar2=None, op0=ALU.mult)
-        nc.vector.transpose(out=re_cols[:], in_=re_rows[:])
-        quantize(w1q, 0, M)
-
-        dst, src = views(xq[0], 0, x_raw, X_SPLIT, N)
-        nc.scalar.copy(out=dst, in_=src)
-        dst, src = views(xq[0], 0, x_raw, 0, HALF)
-        nc.vector.tensor_copy(out=dst, in_=src)
-        dst, src = views(xq[0], 0, x_raw, HALF, X_SPLIT)
-        nc.vector.tensor_copy(out=dst, in_=src)
-        quantize(xq, 0, HALF)
-        quantize(xq, HALF, N)
-        dst, src = views(w2q[0], 0, w2_raw, 0, M)
-        nc.vector.tensor_copy(out=dst, in_=src)
-        dst, src = views(w3oq[0], 0, w3_raw, 0, M)
-        nc.vector.tensor_copy(out=dst, in_=src)
-        quantize(w2q, 0, M)
-        dst, src = views(w3oq[0], M, wo_raw, 0, M)
-        nc.vector.tensor_copy(out=dst, in_=src)
-
-        for g in range(G):
-            product(bank_b[g], g, w1q, 0, xq, True, True)
-        for g in range(G):
-            product(bank_a[g], g, w1q, 0, xq, True, False)
-        for g in range(G):
-            product(bank_a[g], g, w2q, 0, xq, False, True)
-
-        def exp_z(g):
-            nc.scalar.activation(out=e_z[g][:], in_=bank_b[g][:], func=ACT.Exp)
-
-        def exp_d(g):
-            nc.scalar.activation(out=e_d[g][:], in_=bank_a[g][:], func=ACT.Exp)
+        w1_mx = operand("w1", M)
+        w2_mx = operand("w2", M)
+        w3o_mx = operand("w3o", 2 * M)
+        x_mx = operand("x", N)
+        dy_mx = operand("dy", N)
+        z2_c0 = [ps.tile([P, N], F32, name="z2_c0_%d" % g) for g in range(G)]
+        z1_z3 = [ps.tile([P, N], F32, name="z1_z3_%d" % g) for g in range(G)]
+        inv_e1 = per_group("inv_e1")
+        e2 = per_group("e2")
+        odds = per_group("odds")
+        square = per_group("square")
+        share = per_group("share")
+        dev = per_group("dev")
+        with_z3 = per_group("with_z3")
+        with_c0 = per_group("with_c0")
+        result = per_group("result")
+        on_vector = nc.vector.tensor_copy
+        on_scalar = nc.scalar.copy
 
         def make_odds(g):
             nc.vector.scalar_tensor_tensor(
-                out=odds[g][:], in0=e_z[g][:], scalar=re_cols[:, 32 * g : 32 * g + 1], in1=e_d[g][:],
-                op0=ALU.mult, op1=ALU.add)
+                out=odds[g][:], in0=e2[g][:], scalar=re_cols[:, BLOCK * g : BLOCK * g + 1], in1=inv_e1[g][:],
+                op0=ALU.add, op1=ALU.mult,
+            )
 
-        def make_sq(g):
+        def square_less_one(g, cols):
             nc.vector.scalar_tensor_tensor(
-                out=sq[g][:], in0=odds[g][:], scalar=2.0, in1=odds[g][:], op0=ALU.add, op1=ALU.mult)
+                out=square[g][:, cols], in0=odds[g][:, cols], scalar=2.0, in1=odds[g][:, cols],
+                op0=ALU.add, op1=ALU.mult,
+            )
 
-        def cast_dy(h):
-            dst, src = views(dyq[0], 0, dy_raw, h * HALF, (h + 1) * HALF)
-            nc.vector.tensor_copy(out=dst, in_=src)
+        def finish(engine, g, cols):
+            engine.tensor_tensor(
+                out=result[g][:, cols], in0=old_sb[:, g, cols], in1=with_c0[g][:, cols], op=ALU.subtract
+            )
 
-        exp_z(0)
-        exp_z(1)
-        exp_d(0)
-        exp_d(1)
-        exp_z(2)
-        exp_d(2)
-        exp_z(3)
-        exp_d(3)
-        quantize(w3oq, 0, 2 * M)
+        round_to_bf16(on_vector, w1_mx, 0, w1_raw, 0, M)
+        quantize(w1_mx, 0, M)
+        for h in range(2):
+            round_to_bf16(on_scalar, x_mx, h * HALF, x_raw[h], X_VECTOR_COLUMNS, HALF)
+            round_to_bf16(on_vector, x_mx, h * HALF, x_raw[h], 0, X_VECTOR_COLUMNS)
+            quantize(x_mx, h * HALF, (h + 1) * HALF)
+        nc.vector.transpose(out=re_cols[:], in_=re_rows[:])
+        round_to_bf16(on_scalar, w2_mx, 0, w2_raw, 0, M)
+        quantize(w2_mx, 0, M)
+        round_to_bf16(on_vector, w3o_mx, 0, w3_raw, 0, M)
+        round_to_bf16(on_vector, w3o_mx, M, wo_raw, 0, M)
+
+        for g in range(G):
+            product(z1_z3, g, w1_mx, 0, x_mx)
+            nc.scalar.activation(out=inv_e1[g][:], in_=z1_z3[g][:], func=ACT.Exp, scale=-1.0)
+            product(z2_c0, g, w2_mx, 0, x_mx)
+            nc.scalar.activation(out=e2[g][:], in_=z2_c0[g][:], func=ACT.Exp)
+
+        everything = slice(0, N)
+        quantize(w3o_mx, 0, 2 * M)
         make_odds(0)
-        cast_dy(0)
+        square_less_one(0, everything)
         make_odds(1)
-        cast_dy(1)
-        make_sq(0)
-        quantize(dyq, 0, N)
+        round_to_bf16(on_vector, dy_mx, 0, dy_raw, 0, HALF)
         make_odds(2)
-        make_sq(1)
+        round_to_bf16(on_vector, dy_mx, 0, dy_raw, HALF, N)
+        square_less_one(1, everything)
+        quantize(dy_mx, 0, N)
         make_odds(3)
-        make_sq(2)
-        make_sq(3)
-        for g in range(G):
-            product(bank_a[g], g, w3oq, 0, xq, True, True)
-        for g in range(G):
-            product(bank_b[g], g, w3oq, M, dyq, True, True)
+        square_less_one(2, slice(0, HALF))
 
-        halves = [slice(0, HALF), slice(HALF, N)]
-        for g in range(G):
-            for c in halves:
-                nc.scalar.activation(out=share[g][:, c], in_=sq[g][:, c], func=ACT.Abs_reciprocal_sqrt, bias=1.0)
-            for c in halves:
-                nc.scalar.activation(out=dev[g][:, c], in_=share[g][:, c], func=ACT.Square, bias=-0.5)
-            for c in halves:
+        for g in range(2):
+            product(z1_z3, g, w3o_mx, 0, x_mx)
+        for g in range(2):
+            product(z2_c0, g, w3o_mx, M, dy_mx)
+        for g in range(2, G):
+            product(z1_z3, g, w3o_mx, 0, x_mx)
+            product(z2_c0, g, w3o_mx, M, dy_mx)
+
+        count = len(PIECES)
+        first_scalar_square = count - SCALAR_SQUARES
+        first_vector_finish = count - VECTOR_FINISHES
+        for step in range(count + 4):
+            if first_scalar_square <= step < count:
+                g, cols = PIECES[step]
+                nc.scalar.activation(out=square[g][:, cols], in_=odds[g][:, cols], func=ACT.Square, bias=1.0)
+            k = step - 1
+            if 0 <= k < count:
+                g, cols = PIECES[k]
+                nc.scalar.activation(
+                    out=share[g][:, cols], in_=square[g][:, cols], func=ACT.Abs_reciprocal_sqrt,
+                    bias=1.0 if k < first_scalar_square else 0.0,
+                )
+            k = step - 2
+            if 0 <= k < count:
+                g, cols = PIECES[k]
+                nc.scalar.activation(out=dev[g][:, cols], in_=share[g][:, cols], func=ACT.Square, bias=-0.5)
                 nc.vector.scalar_tensor_tensor(
-                    out=m1[g][:, c], in0=dev[g][:, c], scalar=0.25, in1=bank_a[g][:, c],
-                    op0=ALU.subtract, op1=ALU.mult)
-            for c in halves:
-                nc.vector.tensor_tensor(out=m2[g][:, c], in0=m1[g][:, c], in1=bank_b[g][:, c], op=ALU.mult)
-            eng = nc.gpsimd if g < G - 1 else nc.vector
-            for c in halves:
-                eng.tensor_tensor(out=y[g][:, c], in0=old_sb[:, g, c], in1=m2[g][:, c], op=ALU.subtract)
-            nc.sync.dma_start(out=out[g], in_=y[g][:])
+                    out=with_z3[g][:, cols], in0=dev[g][:, cols], scalar=0.25, in1=z1_z3[g][:, cols],
+                    op0=ALU.subtract, op1=ALU.mult,
+                )
+            k = step - 3
+            if 0 <= k < count:
+                g, cols = PIECES[k]
+                nc.vector.tensor_tensor(
+                    out=with_c0[g][:, cols], in0=with_z3[g][:, cols], in1=z2_c0[g][:, cols], op=ALU.mult
+                )
+                if k < first_vector_finish:
+                    if cols.stop % HALF == 0:
+                        finish(nc.gpsimd, g, slice(cols.stop - HALF, cols.stop))
+                    if g >= 2:
+                        nc.sync.dma_start(out=out[g][:, cols], in_=result[g][:, cols])
+                    elif cols.stop == N:
+                        nc.sync.dma_start(out=out[g][:, everything], in_=result[g][:, everything])
+            k = step - 4
+            if first_vector_finish <= k < count:
+                g, cols = PIECES[k]
+                finish(nc.vector, g, cols)
+                nc.scalar.dma_start(out=out[g][:, cols], in_=result[g][:, cols])

from contextlib import ExitStack

import concourse.mybir as mybir

G, D, M, N = 4, 128, 128, 512
FLOPS = 4 * 2 * G * D * M * N

F32 = mybir.dt.float32
BF16 = mybir.dt.bfloat16
U32 = mybir.dt.uint32
U8 = mybir.dt.uint8
FP8X4 = mybir.dt.float8_e4m3fn_x4
ACT = mybir.ActivationFunctionType
ALU = mybir.AluOpType

P = 128
PACK = 4
ROWS = D // PACK
BLOCK = 32
HALF = N // 2
QUARTER = N // 4
X_VECTOR_COLUMNS = 160

PIECES = [(0, slice(0, QUARTER)), (0, slice(QUARTER, HALF)), (0, slice(HALF, N))] + [
    (g, slice(h * HALF, (h + 1) * HALF)) for g in range(1, G) for h in range(2)
]
SCALAR_SQUARES = 3
VECTOR_FINISHES = 2


def tile_rows_btwoshare_kernel(tc, x, w1, w2, w3, re, wo, dy, old, out):
    nc = tc.nc
    with ExitStack() as ctx:
        sb = ctx.enter_context(tc.tile_pool(name="sb", bufs=1))
        ps = ctx.enter_context(tc.psum_pool(name="ps", bufs=1))
        ctx.enter_context(tc.manual_schedule())

        def load(name, src, first, last):
            raw = sb.tile([P, PACK, last - first], F32, name=name + "_raw", align_bytes=64)
            nc.sync.dma_start(out=raw[:], in_=src.rearrange("g (p j) c -> (g p) j c", j=PACK)[:, :, first:last])
            return raw

        def operand(name, width):
            rounded = sb.tile([P, width, PACK], BF16, name=name + "_bf16", align_bytes=64)
            codes = sb.tile([P, width], U32, name=name + "_codes", align_bytes=64)
            scales = sb.tile([P, width], U8, name=name + "_scales", align_bytes=64)
            return rounded, codes, scales

        def round_to_bf16(copy, mx, at, raw, first, last):
            copy(
                out=mx[0][:, at + first : at + last, :].rearrange("p (c i) j -> p c j i", i=2),
                in_=raw[:, :, first:last].rearrange("p j (c i) -> p c j i", i=2),
            )

        def quantize(mx, first, last):
            rounded, codes, scales = mx
            nc.vector.quantize_mx(
                out=codes[:, first:last].bitcast(FP8X4),
                scales=scales[:, first:last],
                in_=rounded[:, first:last, :].rearrange("p c j -> p (c j)"),
            )

        def product(bank, g, weights, at, moving):
            rows = slice(ROWS * g, ROWS * (g + 1))
            nc.tensor.matmul_mx(
                out=bank[g][:],
                lhsT=weights[1][rows, at : at + M].bitcast(FP8X4),
                lhsT_scale=weights[2][rows, at : at + M],
                rhs=moving[1][rows, :].bitcast(FP8X4),
                rhs_scale=moving[2][rows, :],
                start=True,
                stop=True,
            )

        def per_group(name):
            return [sb.tile([P, N], F32, name="%s%d" % (name, g), align_bytes=64) for g in range(G)]

        re_rows = sb.tile([P, G * BLOCK], F32, name="re_rows", align_bytes=64)
        re_cols = sb.tile([P, G * BLOCK], F32, name="re_cols", align_bytes=64)
        nc.gpsimd.memset(re_rows[:], 0.0)
        nc.scalar.dma_start(
            out=re_rows[0:P:BLOCK, :].rearrange("q (g i) -> q g i", g=G),
            in_=re.rearrange("g (q i) o -> q g (i o)", i=BLOCK),
        )

        w1_raw = load("w1", w1, 0, M)
        x_raw = [load("x0", x, 0, HALF), load("x1", x, HALF, N)]
        w2_raw = load("w2", w2, 0, M)
        w3_raw = load("w3", w3, 0, M)
        wo_raw = load("wo", wo, 0, M)
        dy_raw = load("dy", dy, 0, N)
        old_sb = sb.tile([P, G, N], F32, name="old_sb", align_bytes=64)
        nc.sync.dma_start(out=old_sb[:], in_=old.rearrange("g m n -> m g n"))

        w1_mx = operand("w1", M)
        w2_mx = operand("w2", M)
        w3o_mx = operand("w3o", 2 * M)
        x_mx = operand("x", N)
        dy_mx = operand("dy", N)
        z2_c0 = [ps.tile([P, N], F32, name="z2_c0_%d" % g) for g in range(G)]
        z1_z3 = [ps.tile([P, N], F32, name="z1_z3_%d" % g) for g in range(G)]
        inv_e1 = per_group("inv_e1")
        e2 = per_group("e2")
        odds = per_group("odds")
        square = per_group("square")
        share = per_group("share")
        dev = per_group("dev")
        with_z3 = per_group("with_z3")
        with_c0 = per_group("with_c0")
        result = per_group("result")
        on_vector = nc.vector.tensor_copy
        on_scalar = nc.scalar.copy

        def make_odds(g):
            nc.vector.scalar_tensor_tensor(
                out=odds[g][:], in0=e2[g][:], scalar=re_cols[:, BLOCK * g : BLOCK * g + 1], in1=inv_e1[g][:],
                op0=ALU.add, op1=ALU.mult,
            )

        def square_less_one(g, cols):
            nc.vector.scalar_tensor_tensor(
                out=square[g][:, cols], in0=odds[g][:, cols], scalar=2.0, in1=odds[g][:, cols],
                op0=ALU.add, op1=ALU.mult,
            )

        def finish(engine, g, cols):
            engine.tensor_tensor(
                out=result[g][:, cols], in0=old_sb[:, g, cols], in1=with_c0[g][:, cols], op=ALU.subtract
            )

        round_to_bf16(on_vector, w1_mx, 0, w1_raw, 0, M)
        quantize(w1_mx, 0, M)
        for h in range(2):
            round_to_bf16(on_scalar, x_mx, h * HALF, x_raw[h], X_VECTOR_COLUMNS, HALF)
            round_to_bf16(on_vector, x_mx, h * HALF, x_raw[h], 0, X_VECTOR_COLUMNS)
            quantize(x_mx, h * HALF, (h + 1) * HALF)
        nc.vector.transpose(out=re_cols[:], in_=re_rows[:])
        round_to_bf16(on_scalar, w2_mx, 0, w2_raw, 0, M)
        quantize(w2_mx, 0, M)
        round_to_bf16(on_vector, w3o_mx, 0, w3_raw, 0, M)
        round_to_bf16(on_vector, w3o_mx, M, wo_raw, 0, M)

        for g in range(G):
            product(z1_z3, g, w1_mx, 0, x_mx)
            nc.scalar.activation(out=inv_e1[g][:], in_=z1_z3[g][:], func=ACT.Exp, scale=-1.0)
            product(z2_c0, g, w2_mx, 0, x_mx)
            nc.scalar.activation(out=e2[g][:], in_=z2_c0[g][:], func=ACT.Exp)

        everything = slice(0, N)
        quantize(w3o_mx, 0, 2 * M)
        make_odds(0)
        square_less_one(0, everything)
        make_odds(1)
        round_to_bf16(on_vector, dy_mx, 0, dy_raw, 0, HALF)
        make_odds(2)
        round_to_bf16(on_vector, dy_mx, 0, dy_raw, HALF, N)
        square_less_one(1, everything)
        quantize(dy_mx, 0, N)
        make_odds(3)
        square_less_one(2, slice(0, HALF))

        for g in range(2):
            product(z1_z3, g, w3o_mx, 0, x_mx)
        for g in range(2):
            product(z2_c0, g, w3o_mx, M, dy_mx)
        for g in range(2, G):
            product(z1_z3, g, w3o_mx, 0, x_mx)
            product(z2_c0, g, w3o_mx, M, dy_mx)

        count = len(PIECES)
        first_scalar_square = count - SCALAR_SQUARES
        first_vector_finish = count - VECTOR_FINISHES
        for step in range(count + 4):
            if first_scalar_square <= step < count:
                g, cols = PIECES[step]
                nc.scalar.activation(out=square[g][:, cols], in_=odds[g][:, cols], func=ACT.Square, bias=1.0)
            k = step - 1
            if 0 <= k < count:
                g, cols = PIECES[k]
                nc.scalar.activation(
                    out=share[g][:, cols], in_=square[g][:, cols], func=ACT.Abs_reciprocal_sqrt,
                    bias=1.0 if k < first_scalar_square else 0.0,
                )
            k = step - 2
            if 0 <= k < count:
                g, cols = PIECES[k]
                nc.scalar.activation(out=dev[g][:, cols], in_=share[g][:, cols], func=ACT.Square, bias=-0.5)
                nc.vector.scalar_tensor_tensor(
                    out=with_z3[g][:, cols], in0=dev[g][:, cols], scalar=0.25, in1=z1_z3[g][:, cols],
                    op0=ALU.subtract, op1=ALU.mult,
                )
            k = step - 3
            if 0 <= k < count:
                g, cols = PIECES[k]
                nc.vector.tensor_tensor(
                    out=with_c0[g][:, cols], in0=with_z3[g][:, cols], in1=z2_c0[g][:, cols], op=ALU.mult
                )
                if k < first_vector_finish:
                    if cols.stop % HALF == 0:
                        finish(nc.gpsimd, g, slice(cols.stop - HALF, cols.stop))
                    if g >= 2:
                        nc.sync.dma_start(out=out[g][:, cols], in_=result[g][:, cols])
                    elif cols.stop == N:
                        nc.sync.dma_start(out=out[g][:, everything], in_=result[g][:, everything])
            k = step - 4
            if first_vector_finish <= k < count:
                g, cols = PIECES[k]
                finish(nc.vector, g, cols)
                nc.scalar.dma_start(out=out[g][:, cols], in_=result[g][:, cols])
